import numpy as np
import ml_dtypes

BF16 = ml_dtypes.bfloat16


def bf(x):
    return np.asarray(x, np.float32).astype(BF16)


def f32(x):
    return np.asarray(x, np.float32)


def f64(x):
    return np.asarray(x).astype(np.float64)


def striped(idx):
    return np.tile(idx.reshape(-1, 16).T, (8, 1))


def rows(idx, k):
    return np.tile(idx, (k, 1))


def look(tab, idx):
    return np.take_along_axis(f64(tab), rows(idx, len(tab)), axis=1)


K, S, V, N, M = 128, 2048, 512, 512, 256


def silu(v):
    return v / (1.0 + np.exp(-v))


def setup_inputs():
    return {"tab": f32(np.random.standard_normal((2, K, S))), "y": f32(np.random.standard_normal((K, V))), "w": bf(np.random.standard_normal((K, M)) / np.sqrt(K)), "b": f32(0.5 * np.random.standard_normal((M, 1))), "offs": striped(np.random.permutation(S)[:N])}


def reference(tab, y, w, b, offs):
    idx = offs[:16].T.reshape(-1)
    x = (look(tab[0], idx) * f64(y)) * (silu(look(tab[1], idx)))
    return np.maximum(f64(w).T @ x + f64(b), 0.0)

@@ -1,0 +1,44 @@
+import concourse.mybir as mybir
+
+P, S, N, M = 128, 2048, 512, 256
+BLOCKS = M // P
+FLOPS = 2 * P * M * N
+
+F32, BF16, U16 = mybir.dt.float32, mybir.dt.bfloat16, mybir.dt.uint16
+ALU = mybir.AluOpType
+ACT = mybir.ActivationFunctionType
+
+
+def tile_lookup_vg_mulsilu_relu_kernel(tc, tab, y, w, b, offs, out):
+    nc = tc.nc
+    with (
+        tc.tile_pool(name="sbuf", bufs=1) as sbuf,
+        tc.psum_pool(name="psum", bufs=1) as psum,
+    ):
+        offsets = sbuf.tile([P, N // 16], U16, name="offsets")
+        gates = sbuf.tile([P, S], F32, name="gates")
+        values = sbuf.tile([P, S], F32, name="values")
+        stream = sbuf.tile([P, N], F32, name="stream")
+        weights = sbuf.tile([P, P, BLOCKS], BF16, name="weights")
+        bias = sbuf.tile([P, BLOCKS], F32, name="bias")
+
+        nc.sync.dma_start(offsets[:], offs)
+        nc.sync.dma_start(gates[:], tab[1])
+        nc.sync.dma_start(stream[:], y)
+        nc.sync.dma_start(values[:], tab[0])
+        nc.sync.dma_start(weights[:], w.rearrange("r (p h) -> r p h", h=BLOCKS))
+        nc.sync.dma_start(bias[:], b.rearrange("(p h) o -> p (h o)", h=BLOCKS))
+
+        gate = sbuf.tile([P, N], F32, name="gate")
+        nc.scalar.activation(gate[:], gates[:].indirect(offsets[:]), ACT.Silu)
+        scaled = sbuf.tile([P, N], F32, name="scaled")
+        nc.vector.tensor_tensor(scaled[:], values[:].indirect(offsets[:]), stream[:], ALU.mult)
+        x = sbuf.tile([P, N], BF16, name="x")
+        nc.vector.tensor_tensor(x[:], scaled[:], gate[:], ALU.mult)
+
+        result = sbuf.tile([P, BLOCKS, N], F32, name="result")
+        for h in range(BLOCKS):
+            product = psum.tile([P, N], F32, name=f"product{h}")
+            nc.tensor.matmul(product[:], weights[:, :, h], x[:], start=True, stop=True)
+            nc.scalar.activation(result[:, h, :], product[:], ACT.Relu, bias=bias[:, h : h + 1])
+        nc.sync.dma_start(out.rearrange("(p h) i -> p h i", h=BLOCKS), result[:])

@@ -2,6 +2,8 @@ import concourse.mybir as mybir
 
 P, S, N, M = 128, 2048, 512, 256
 BLOCKS = M // P
+PIECES = 4
+WIDTH = N // PIECES
 FLOPS = 2 * P * M * N
 
 F32, BF16, U16 = mybir.dt.float32, mybir.dt.bfloat16, mybir.dt.uint16
@@ -22,23 +24,46 @@ def tile_lookup_vg_mulsilu_relu_kernel(tc, tab, y, w, b, offs, out):
         weights = sbuf.tile([P, P, BLOCKS], BF16, name="weights")
         bias = sbuf.tile([P, BLOCKS], F32, name="bias")
 
-        nc.sync.dma_start(offsets[:], offs)
         nc.sync.dma_start(gates[:], tab[1])
-        nc.sync.dma_start(stream[:], y)
-        nc.sync.dma_start(values[:], tab[0])
-        nc.sync.dma_start(weights[:], w.rearrange("r (p h) -> r p h", h=BLOCKS))
+        nc.sync.dma_start(offsets[:], offs)
         nc.sync.dma_start(bias[:], b.rearrange("(p h) o -> p (h o)", h=BLOCKS))
+        nc.sync.dma_start(stream[:, : N // 2], y[:, : N // 2])
+        nc.sync.dma_start(values[:], tab[0])
+        nc.sync.dma_start(stream[:, N // 2 :], y[:, N // 2 :])
+        nc.sync.dma_start(weights[:], w.rearrange("r (p h) -> r p h", h=BLOCKS))
+
+        zeros = sbuf.tile([P, 8], F32, name="zeros")
+        nc.vector.memset(zeros[:], 0.0)
+        warm = sbuf.tile([P, 8], F32, name="warm")
+        nc.scalar.activation(warm[:], zeros[:], ACT.Silu)
 
         gate = sbuf.tile([P, N], F32, name="gate")
         nc.scalar.activation(gate[:], gates[:].indirect(offsets[:]), ACT.Silu)
-        scaled = sbuf.tile([P, N], F32, name="scaled")
-        nc.vector.tensor_tensor(scaled[:], values[:].indirect(offsets[:]), stream[:], ALU.mult)
-        x = sbuf.tile([P, N], BF16, name="x")
-        nc.vector.tensor_tensor(x[:], scaled[:], gate[:], ALU.mult)
 
-        result = sbuf.tile([P, BLOCKS, N], F32, name="result")
-        for h in range(BLOCKS):
-            product = psum.tile([P, N], F32, name=f"product{h}")
-            nc.tensor.matmul(product[:], weights[:, :, h], x[:], start=True, stop=True)
-            nc.scalar.activation(result[:, h, :], product[:], ACT.Relu, bias=bias[:, h : h + 1])
-        nc.sync.dma_start(out.rearrange("(p h) i -> p h i", h=BLOCKS), result[:])
+        scaled = sbuf.tile([P, N], F32, name="scaled")
+        x = sbuf.tile([P, N], BF16, name="x")
+        result = sbuf.tile([P, PIECES, BLOCKS, WIDTH], F32, name="result")
+        out_rows = out.rearrange("(p h) i -> p h i", h=BLOCKS)
+
+        def look_up(k):
+            cols = slice(k * WIDTH, (k + 1) * WIDTH)
+            picked = values[:].indirect(offsets[:, k * WIDTH // 16 : (k + 1) * WIDTH // 16])
+            nc.vector.tensor_tensor(scaled[:, cols], picked, stream[:, cols], ALU.mult)
+
+        def layer(k):
+            cols = slice(k * WIDTH, (k + 1) * WIDTH)
+            nc.vector.tensor_tensor(x[:, cols], scaled[:, cols], gate[:, cols], ALU.mult)
+            for h in range(BLOCKS):
+                product = psum.tile([P, WIDTH], F32, name=f"product{k}_{h}")
+                nc.tensor.matmul(product[:], weights[:, :, h], x[:, cols], start=True, stop=True)
+                if k == PIECES - 1 and h == 0:
+                    nc.vector.tensor_scalar(result[:, k, h, :], product[:], bias[:, h : h + 1], 0.0, ALU.add, ALU.max)
+                else:
+                    nc.scalar.activation(result[:, k, h, :], product[:], ACT.Relu, bias=bias[:, h : h + 1])
+            nc.sync.dma_start(out_rows[:, :, cols], result[:, k])
+
+        look_up(0)
+        for k in range(1, PIECES):
+            look_up(k)
+            layer(k - 1)
+        layer(PIECES - 1)

@@ -2,8 +2,10 @@ import concourse.mybir as mybir
 
 P, S, N, M = 128, 2048, 512, 256
 BLOCKS = M // P
-PIECES = 4
-WIDTH = N // PIECES
+WIDTH = 128
+PIECES = [slice(start, start + WIDTH) for start in range(0, N, WIDTH)]
+BANK = 512
+WARM_UPS = 3
 FLOPS = 2 * P * M * N
 
 F32, BF16, U16 = mybir.dt.float32, mybir.dt.bfloat16, mybir.dt.uint16
@@ -15,7 +17,7 @@ def tile_lookup_vg_mulsilu_relu_kernel(tc, tab, y, w, b, offs, out):
     nc = tc.nc
     with (
         tc.tile_pool(name="sbuf", bufs=1) as sbuf,
-        tc.psum_pool(name="psum", bufs=1) as psum,
+        tc.psum_pool(name="psum", bufs=4) as psum,
     ):
         offsets = sbuf.tile([P, N // 16], U16, name="offsets")
         gates = sbuf.tile([P, S], F32, name="gates")
@@ -26,44 +28,52 @@ def tile_lookup_vg_mulsilu_relu_kernel(tc, tab, y, w, b, offs, out):
 
         nc.sync.dma_start(gates[:], tab[1])
         nc.sync.dma_start(offsets[:], offs)
-        nc.sync.dma_start(bias[:], b.rearrange("(p h) o -> p (h o)", h=BLOCKS))
+        nc.scalar.dma_start(bias[:], b.rearrange("(p h) o -> p (h o)", h=BLOCKS))
         nc.sync.dma_start(stream[:, : N // 2], y[:, : N // 2])
         nc.sync.dma_start(values[:], tab[0])
         nc.sync.dma_start(stream[:, N // 2 :], y[:, N // 2 :])
         nc.sync.dma_start(weights[:], w.rearrange("r (p h) -> r p h", h=BLOCKS))
 
-        zeros = sbuf.tile([P, 8], F32, name="zeros")
+        zeros = sbuf.tile([P, P], F32, name="zeros")
         nc.vector.memset(zeros[:], 0.0)
         warm = sbuf.tile([P, 8], F32, name="warm")
-        nc.scalar.activation(warm[:], zeros[:], ACT.Silu)
+        nc.scalar.activation(warm[:], zeros[:, :8], ACT.Silu)
+        idle = psum.tile([P, BANK], F32, name="idle", tag="block1")
+        for turn in range(WARM_UPS):
+            nc.tensor.matmul(idle[:, : N // 2], zeros[:], stream[:, : N // 2], start=True, stop=True)
 
         gate = sbuf.tile([P, N], F32, name="gate")
         nc.scalar.activation(gate[:], gates[:].indirect(offsets[:]), ACT.Silu)
 
         scaled = sbuf.tile([P, N], F32, name="scaled")
         x = sbuf.tile([P, N], BF16, name="x")
-        result = sbuf.tile([P, PIECES, BLOCKS, WIDTH], F32, name="result")
+        result = sbuf.tile([P, BLOCKS, N], F32, name="result")
         out_rows = out.rearrange("(p h) i -> p h i", h=BLOCKS)
 
-        def look_up(k):
-            cols = slice(k * WIDTH, (k + 1) * WIDTH)
-            picked = values[:].indirect(offsets[:, k * WIDTH // 16 : (k + 1) * WIDTH // 16])
+        def look_up(cols):
+            picked = values[:].indirect(offsets[:, cols.start // 16 : cols.stop // 16])
             nc.vector.tensor_tensor(scaled[:, cols], picked, stream[:, cols], ALU.mult)
 
-        def layer(k):
-            cols = slice(k * WIDTH, (k + 1) * WIDTH)
+        def apply_gate(cols):
             nc.vector.tensor_tensor(x[:, cols], scaled[:, cols], gate[:, cols], ALU.mult)
-            for h in range(BLOCKS):
-                product = psum.tile([P, WIDTH], F32, name=f"product{k}_{h}")
-                nc.tensor.matmul(product[:], weights[:, :, h], x[:, cols], start=True, stop=True)
-                if k == PIECES - 1 and h == 0:
-                    nc.vector.tensor_scalar(result[:, k, h, :], product[:], bias[:, h : h + 1], 0.0, ALU.add, ALU.max)
-                else:
-                    nc.scalar.activation(result[:, k, h, :], product[:], ACT.Relu, bias=bias[:, h : h + 1])
-            nc.sync.dma_start(out_rows[:, :, cols], result[:, k])
 
-        look_up(0)
-        for k in range(1, PIECES):
-            look_up(k)
-            layer(k - 1)
-        layer(PIECES - 1)
+        def layer(cols, vector_is_free):
+            for h in range(BLOCKS):
+                bank = psum.tile([P, BANK], F32, name="bank", tag=f"block{h}")
+                product = bank[:, : cols.stop - cols.start]
+                nc.tensor.matmul(product, weights[:, :, h], x[:, cols], start=True, stop=True)
+                if vector_is_free and h == 0:
+                    nc.vector.tensor_scalar(result[:, h, cols], product, bias[:, h : h + 1], 0.0, ALU.add, ALU.max)
+                else:
+                    nc.scalar.activation(result[:, h, cols], product, ACT.Relu, bias=bias[:, h : h + 1])
+            nc.sync.dma_start(out_rows[:, :, cols], result[:, :, cols])
+
+        look_up(PIECES[0])
+        for ahead, cols in zip(PIECES[1:], PIECES):
+            look_up(ahead)
+            apply_gate(cols)
+            if ahead != PIECES[-1]:
+                layer(cols, False)
+        apply_gate(PIECES[-1])
+        for cols in PIECES[-2:]:
+            layer(cols, True)

import concourse.mybir as mybir

P, S, N, M = 128, 2048, 512, 256
BLOCKS = M // P
WIDTH = 128
PIECES = [slice(start, start + WIDTH) for start in range(0, N, WIDTH)]
BANK = 512
WARM_UPS = 3
FLOPS = 2 * P * M * N

F32, BF16, U16 = mybir.dt.float32, mybir.dt.bfloat16, mybir.dt.uint16
ALU = mybir.AluOpType
ACT = mybir.ActivationFunctionType


def tile_lookup_vg_mulsilu_relu_kernel(tc, tab, y, w, b, offs, out):
    nc = tc.nc
    with (
        tc.tile_pool(name="sbuf", bufs=1) as sbuf,
        tc.psum_pool(name="psum", bufs=4) as psum,
    ):
        offsets = sbuf.tile([P, N // 16], U16, name="offsets")
        gates = sbuf.tile([P, S], F32, name="gates")
        values = sbuf.tile([P, S], F32, name="values")
        stream = sbuf.tile([P, N], F32, name="stream")
        weights = sbuf.tile([P, P, BLOCKS], BF16, name="weights")
        bias = sbuf.tile([P, BLOCKS], F32, name="bias")

        nc.sync.dma_start(gates[:], tab[1])
        nc.sync.dma_start(offsets[:], offs)
        nc.scalar.dma_start(bias[:], b.rearrange("(p h) o -> p (h o)", h=BLOCKS))
        nc.sync.dma_start(stream[:, : N // 2], y[:, : N // 2])
        nc.sync.dma_start(values[:], tab[0])
        nc.sync.dma_start(stream[:, N // 2 :], y[:, N // 2 :])
        nc.sync.dma_start(weights[:], w.rearrange("r (p h) -> r p h", h=BLOCKS))

        zeros = sbuf.tile([P, P], F32, name="zeros")
        nc.vector.memset(zeros[:], 0.0)
        warm = sbuf.tile([P, 8], F32, name="warm")
        nc.scalar.activation(warm[:], zeros[:, :8], ACT.Silu)
        idle = psum.tile([P, BANK], F32, name="idle", tag="block1")
        for turn in range(WARM_UPS):
            nc.tensor.matmul(idle[:, : N // 2], zeros[:], stream[:, : N // 2], start=True, stop=True)

        gate = sbuf.tile([P, N], F32, name="gate")
        nc.scalar.activation(gate[:], gates[:].indirect(offsets[:]), ACT.Silu)

        scaled = sbuf.tile([P, N], F32, name="scaled")
        x = sbuf.tile([P, N], BF16, name="x")
        result = sbuf.tile([P, BLOCKS, N], F32, name="result")
        out_rows = out.rearrange("(p h) i -> p h i", h=BLOCKS)

        def look_up(cols):
            picked = values[:].indirect(offsets[:, cols.start // 16 : cols.stop // 16])
            nc.vector.tensor_tensor(scaled[:, cols], picked, stream[:, cols], ALU.mult)

        def apply_gate(cols):
            nc.vector.tensor_tensor(x[:, cols], scaled[:, cols], gate[:, cols], ALU.mult)

        def layer(cols, vector_is_free):
            for h in range(BLOCKS):
                bank = psum.tile([P, BANK], F32, name="bank", tag=f"block{h}")
                product = bank[:, : cols.stop - cols.start]
                nc.tensor.matmul(product, weights[:, :, h], x[:, cols], start=True, stop=True)
                if vector_is_free and h == 0:
                    nc.vector.tensor_scalar(result[:, h, cols], product, bias[:, h : h + 1], 0.0, ALU.add, ALU.max)
                else:
                    nc.scalar.activation(result[:, h, cols], product, ACT.Relu, bias=bias[:, h : h + 1])
            nc.sync.dma_start(out_rows[:, :, cols], result[:, :, cols])

        look_up(PIECES[0])
        for ahead, cols in zip(PIECES[1:], PIECES):
            look_up(ahead)
            apply_gate(cols)
            if ahead != PIECES[-1]:
                layer(cols, False)
        apply_gate(PIECES[-1])
        for cols in PIECES[-2:]:
            layer(cols, True)
